import numpy as np, ml_dtypes
CORES = [76,84,92,100,108,116,124]
N = 7
import mx_ref
NC, G = 128, 4
C = np.float32(0.00048828125)
BF = ml_dtypes.bfloat16
def cut(t, i, w=512):
    return t[:, w * i:w * i + w]
def tile(rs):
    return np.stack(rs, axis=2).reshape(128, -1).astype(BF)
def layer(w, X):
    out = []
    for i in range(G):
        for t in range(len(X)):
            p = mx_ref.matmul(mx_ref.quantize(cut(w, len(X) * i + t)), X[t])
            z = p if t == 0 else z + p
        out.append(z)
    return out
def gate(U, V):
    return [(np.maximum(u, 0) * v) * C for u, v in zip(U, V)]
def setup_inputs(rng):
    def f(*shape):
        return mx_ref.flush((rng.standard_normal(shape, dtype=np.float32) * np.exp2(rng.integers(-2, 3, shape[:-1] + (1,)))).astype(BF))
    return {"x": f(N, 128, 4 * NC), "u": f(N, 128, G * 512), "v": f(N, 128, G * 512), "w2": f(N, 128, N * 512)}
def setup_inputs_blocks(rng):
    d = setup_inputs(rng)
    for k in ("x", "u", "v", "w2"): d[k] = mx_ref.spread(d[k], rng, 2)
    return d
def setup_inputs_wide(rng):
    d = setup_inputs(rng)
    for k in ("x", "u", "v", "w2"): d[k] = mx_ref.flush((d[k].astype(np.float32) * np.exp2(rng.integers(-5, 6, (N, 1, 1))).astype(np.float32)).astype(BF))
    return d
def setup_inputs_zeros(rng):
    d = setup_inputs(rng); v = d["x"].reshape(N, 128, -1, 4).copy()
    v[np.broadcast_to((rng.random((N, 1, v.shape[2], 1)) < 0.33), v.shape)] = 0
    d["x"] = v.reshape(d["x"].shape)
    return d
def reference(x, u, v, w2):
    h = np.zeros((N, 128, 4 * NC), BF)
    for j in range(N):
        X = [mx_ref.quantize(x[j])]
        h[j] = tile(gate(layer(u[j], X), layer(v[j], X)))
    H = [mx_ref.quantize(h[j]) for j in range(N)]
    y = np.zeros((N, 128, NC), np.float32)
    for r in range(N):
        for j in range(N):
            p = mx_ref.matmul(mx_ref.quantize(cut(w2[r], j)), H[j])
            y[r] = p if j == 0 else y[r] + p
    return {"y": y}

from concourse.bass import DstId, RemoteDMATransfer
from concourse.mybir import dt, AluOpType, ActivationFunctionType

N = 7
NC = 128
G = 4
TW = 4 * NC
SCALE = 0.00048828125
DIRECT = 2
WA = 4

SCRATCH = {
    "xb": ("sbuf", [128, TW], "bfloat16"),
    "ub": ("sbuf", [128, G * TW], "bfloat16"),
    "vb": ("sbuf", [128, G * TW], "bfloat16"),
    "wb": ("sbuf", [128, N * TW], "bfloat16"),
    "hb": ("sbuf", [128, TW], "bfloat16"),
    "xq": ("sbuf", [128, NC], "float8_e4m3fn_x4"),
    "xs": ("sbuf", [128, NC], "uint8"),
    "uq": ("sbuf", [128, G * NC], "float8_e4m3fn_x4"),
    "us": ("sbuf", [128, G * NC], "uint8"),
    "vq": ("sbuf", [128, G * NC], "float8_e4m3fn_x4"),
    "vs": ("sbuf", [128, G * NC], "uint8"),
    "wq": ("sbuf", [128, N * NC], "float8_e4m3fn_x4"),
    "ws": ("sbuf", [128, N * NC], "uint8"),
    "hq": ("sbuf", [128, N * NC], "float8_e4m3fn_x4"),
    "hs": ("sbuf", [128, N * NC], "uint8"),
    "ra": ("sbuf", [128, G * NC], "float32"),
    "yb": ("sbuf", [128, NC], "float32"),
    "pu": ("psum", [128, G * 512], "float32"),
    "pv": ("psum", [128, G * 512], "float32"),
}
SEMAPHORES = (["ld_x", "ld_u", "ld_v0", "ld_v1", "ld_wa", "ld_wb", "st_y", "q_x", "q_h", "q_wa", "q_wb", "mul", "mm_y",
               "cp_y", "hin", "sent"]
              + ["q_u%d" % i for i in range(G)] + ["q_v%d" % i for i in range(G)]
              + ["mm_u%d" % i for i in range(G)] + ["mm_v%d" % i for i in range(G)]
              + ["rl%d" % i for i in range(G)] + ["arr%d" % j for j in range(N)])


def _engines(mask):
    return [e for e in range(mask.bit_length()) if (mask >> e) & 1]


def _bits(engines):
    m = 0
    for e in engines:
        m |= 1 << e
    return m


def _halves(engines):
    h = len(engines) // 2
    return [engines[:h], engines[h:]]


def _plan(cores, topo):
    every = range(topo.CHIPS * topo.CORES_PER_CHIP)
    landed = {}
    plan = {}
    for s in cores:
        near = [d for d in cores if d != s and topo.may_write(s, d)]
        far = [d for d in cores if d != s and not topo.may_write(s, d)]
        ring = sorted(near + [s])
        i = ring.index(s)
        turn = ring[i + 1:] + ring[:i]
        direct, rel = turn[:DIRECT], far + turn[DIRECT:]
        owners = [k for k in every if topo.chip(k) == topo.chip(s) and k not in cores
                  and all(topo.may_write(k, d) for d in rel)]
        here = [k for k in owners if topo.die(k) == topo.die(s)]
        there = [k for k in owners if topo.die(k) != topo.die(s)]
        best = None
        for a in range(len(rel)):
            for b in range(a + 1, len(rel)):
                g0 = [rel[a], rel[b]]
                g1 = [d for d in rel if d not in g0]
                trial = dict(landed)
                for grp, k in ((g0, here[0]), (g1, there[0])):
                    for d in grp:
                        trial[(d, topo.die(k))] = trial.get((d, topo.die(k)), 0) + 1
                key = (max(trial.values()), sum(v * v for v in trial.values()))
                if best is None or key < best[0]:
                    best = (key, g0, g1, trial)
        g0, g1, landed = best[1], best[2], best[3]
        plan[s] = {"direct": direct,
                   "relay": [(here[0], "c", g0), (there[0], "c", g1), (here[1], "p", g1), (there[1], "p", g0)]}
    return plan


def _piece(T, kind, j):
    if kind == "c":
        return T.hq[:, NC * j:NC * j + NC].bitcast(dt.uint8)
    return T.hs[:, NC * j:NC * j + NC]


def _send(g, T, topo, kind, j, targets, sem):
    transfers = []
    for dst, engines in targets:
        a = topo.addr(dst)
        transfers.append(RemoteDMATransfer(dst_ids=[DstId(rid=a[0], pnc=a[1])], dma_engine_mask=_bits(engines),
                                           remote_sem=sem, src=_piece(T, kind, j), dst=_piece(T, kind, j)))
    g.remote_dma_fused(transfers, local_sem=T.sem.sent)
    return sum(len(engines) for dst, engines in targets)


def _relay(g, core, T, topo, plan):
    for s in plan:
        for k, kind, dests in plan[s]["relay"]:
            if k != core:
                continue
            j = T.rank_of(s)
            got = len(_halves(_engines(topo.mask(s, k) & topo.mask(s, dests[0])))[0])
            g.wait_ge(T.sem.hin, got)
            parts = _halves(_engines(topo.mask(core, dests[0]) & topo.mask(core, dests[1])))
            n = _send(g, T, topo, kind, j, list(zip(dests, parts)), T.sem["arr%d" % j])
            g.wait_ge(T.sem.sent, n)


def rank_program(g, core, T, topo):
    cores = list(T.cores)
    plan = _plan(cores, topo)
    rank = T.rank_of(core)
    if rank is None:
        _relay(g, core, T, topo, plan)
        return
    S = T.sem
    mine = plan[core]

    g.sync.dma_start(T.xb[:], T.x[:]).then_inc(S.ld_x, 16)
    g.scalar.dma_start(T.ub[:], T.u[:]).then_inc(S.ld_u, 16)
    half = G * TW // 2
    g.sync.dma_start(T.vb[:, 0:half], T.v[:, 0:half]).then_inc(S.ld_v0, 16)
    g.scalar.dma_start(T.vb[:, half:2 * half], T.v[:, half:2 * half]).then_inc(S.ld_v1, 16)
    g.sync.dma_start(T.wb[:, 0:WA * TW], T.w2[:, 0:WA * TW]).then_inc(S.ld_wa, 16)
    g.scalar.dma_start(T.wb[:, WA * TW:N * TW], T.w2[:, WA * TW:N * TW]).then_inc(S.ld_wb, 16)

    V = g.vector
    V.wait_ge(S.ld_x, 16)
    V.quantize_mx(T.xq[:], T.xs[:], T.xb[:]).then_inc(S.q_x, 1)
    V.wait_ge(S.ld_u, 16)
    for i in range(G):
        V.quantize_mx(T.uq[:, NC * i:NC * i + NC], T.us[:, NC * i:NC * i + NC],
                      T.ub[:, TW * i:TW * i + TW]).then_inc(S["q_u%d" % i], 1)
    for part, sem in ((range(0, G // 2), S.ld_v0), (range(G // 2, G), S.ld_v1)):
        V.wait_ge(sem, 16)
        for i in part:
            V.quantize_mx(T.vq[:, NC * i:NC * i + NC], T.vs[:, NC * i:NC * i + NC],
                          T.vb[:, TW * i:TW * i + TW]).then_inc(S["q_v%d" % i], 1)
        for i in part:
            V.wait_ge(S["rl%d" % i], 1)
            V.wait_ge(S["mm_v%d" % i], 1)
            V.tensor_tensor(T.hb[:, i:TW:G], T.ra[:, NC * i:NC * i + NC], T.pv[:, 512 * i:512 * i + NC],
                            AluOpType.mult).then_inc(S.mul, 1)
    V.wait_ge(S.mul, G)
    V.quantize_mx(T.hq[:, NC * rank:NC * rank + NC], T.hs[:, NC * rank:NC * rank + NC], T.hb[:]).then_inc(S.q_h, 1)
    V.wait_ge(S.ld_wa, 16)
    V.quantize_mx(T.wq[:, 0:WA * NC], T.ws[:, 0:WA * NC], T.wb[:, 0:WA * TW]).then_inc(S.q_wa, 1)
    V.wait_ge(S.ld_wb, 16)
    V.quantize_mx(T.wq[:, WA * NC:N * NC], T.ws[:, WA * NC:N * NC], T.wb[:, WA * TW:N * TW]).then_inc(S.q_wb, 1)
    V.wait_ge(S.mm_y, 1)
    V.tensor_copy(T.yb[:], T.pu[:, 0:NC]).then_inc(S.cp_y, 1)

    for i in range(G):
        g.scalar.wait_ge(S["mm_u%d" % i], 1)
        g.scalar.activation(T.ra[:, NC * i:NC * i + NC], T.pu[:, 512 * i:512 * i + NC], ActivationFunctionType.Relu,
                            scale=SCALE).then_inc(S["rl%d" % i], 1)

    relays = mine["relay"]
    off = topo.mask(core, mine["direct"][0])
    stay = topo.mask(core, relays[0][0]) & ~off
    g.wait_ge(S.q_h, 1)
    n = _send(g, T, topo, "c", rank, list(zip([k for k, kind, d in relays if kind == "c"], _halves(_engines(stay)))), S.hin)
    n += _send(g, T, topo, "p", rank, list(zip([k for k, kind, d in relays if kind == "p"], _halves(_engines(off)))), S.hin)
    for kind in ("p", "c"):
        n += _send(g, T, topo, kind, rank, list(zip(mine["direct"], _halves(_engines(off)))), S["arr%d" % rank])
    g.wait_ge(S.sent, n)

    P = g.tensor
    P.wait_ge(S.q_x, 1)
    for name, q, s, ps in (("u", T.uq, T.us, T.pu), ("v", T.vq, T.vs, T.pv)):
        for i in range(G):
            P.wait_ge(S["q_%s%d" % (name, i)], 1)
            P.matmul_mx(ps[:, 512 * i:512 * i + NC], q[:, NC * i:NC * i + NC], s[:, NC * i:NC * i + NC],
                        T.xq[:], T.xs[:], True, True).then_inc(S["mm_%s%d" % (name, i)], 1)
    order = ([core] + [s for s in cores if core in plan[s]["direct"]]
             + [s for s in cores if s != core and core not in plan[s]["direct"]])
    per_piece = len(_halves(_engines(off))[0])
    P.wait_ge(S.rl0, 1)
    P.wait_ge(S.q_h, 1)
    P.wait_ge(S.q_wa, 1)
    P.wait_ge(S.q_wb, 1)
    for t, s in enumerate(order):
        j = T.rank_of(s)
        if s != core:
            P.wait_ge(S["arr%d" % j], 2 * per_piece)
        mm = P.matmul_mx(T.pu[:, 0:NC], T.wq[:, NC * j:NC * j + NC], T.ws[:, NC * j:NC * j + NC],
                         T.hq[:, NC * j:NC * j + NC], T.hs[:, NC * j:NC * j + NC], t == 0, t == N - 1)
    mm.then_inc(S.mm_y, 1)

    g.sync.wait_ge(S.cp_y, 1)
    g.sync.dma_start(T.y[:], T.yb[:]).then_inc(S.st_y, 16)
    g.sync.wait_ge(S.st_y, 16)
